import numpy as np
import ml_dtypes


def mxq(x, axis, fmt="e4m3"):
    dtype, down = {"e4m3": (ml_dtypes.float8_e4m3fn, 7), "e5m2": (ml_dtypes.float8_e5m2, 14)}[fmt]
    v = np.moveaxis(np.asarray(x, np.float32).astype(ml_dtypes.bfloat16).astype(np.float64), axis, -1)
    blocks = v.reshape(v.shape[:-1] + (-1, 32))
    amax = np.abs(blocks).max(-1, keepdims=True)
    byte = np.maximum(np.where(amax > 0, np.frexp(amax)[1] - 1 + 127, 0) - down, 1)
    scale = np.exp2(byte - 127.0)
    codes = (blocks / scale).astype(np.float32).astype(dtype).astype(np.float64)
    return np.moveaxis((codes * scale).reshape(v.shape), -1, axis)


WIDE = False


def mx_kscale(k):
    if not WIDE:
        return np.ones(k)
    levels = np.array([10, -10, 5, -5, 0])
    if k % 512:
        return np.exp2(np.random.permutation(np.resize(levels, k // 32))).repeat(32)
    a = np.empty((k // 512, 16))
    for p in range(k // 512):
        a[p, :8] = np.random.permutation(np.resize(levels, 8))
        for g in range(8):
            far = levels[np.abs(levels - a[p, g]) >= 10]
            a[p, g + 8] = far[np.random.randint(len(far))]
    return np.exp2(a.ravel()).repeat(32)


def f64(x):
    return np.asarray(x).astype(np.float64)


def striped(idx):
    return np.tile(idx.reshape(-1, 16).T, (8, 1)).astype(np.uint16)


def unstriped(offs):
    return offs[:16].T.reshape(-1).astype(np.int64)


def silu(v):
    return v / (1.0 + np.exp(-np.maximum(v, -700.0)))


K, T, D, S, V, R, N = 1536, 1024, 4, 1024, 256, 4, 512


def setup_inputs():
    n = np.random.standard_normal
    s = mx_kscale(K)[:, None]
    return {
        "xT": (n((K, T)) * s).astype(np.float32),
        "w": (n((D, K, N)) / np.sqrt(D * K) / s[None]).astype(np.float32),
        "b": (0.3 * n((N, 1))).astype(np.float32),
        "offs": striped(np.concatenate([R * np.arange(V) + np.random.randint(0, R, V) for _ in range(D)])),
    }


def reference(xT, w, b, offs):
    idx = unstriped(offs)
    xq = mxq(f64(xT)[:, idx], 0, "e4m3")
    wq = mxq(f64(w), 1, "e4m3")
    y = sum(wq[d].T @ xq[:, d * V:(d + 1) * V] for d in range(D))
    y = silu(y + f64(b))
    return y

@@ -1,0 +1,175 @@
+from contextlib import ExitStack
+
+import concourse.mybir as mybir
+
+K, T, D, V, N = 1536, 1024, 4, 256, 512
+FLOPS = 2 * D * K * N * V
+
+F32 = mybir.dt.float32
+BF16 = mybir.dt.bfloat16
+U32 = mybir.dt.uint32
+U16 = mybir.dt.uint16
+U8 = mybir.dt.uint8
+FP8X4 = mybir.dt.float8_e4m3fn_x4
+ACT = mybir.ActivationFunctionType
+
+P = 128
+PACK = 4
+K_PASS = P * PACK
+PASSES = K // K_PASS
+M_TILES = N // P
+RUN = 4
+PAIR = 2 * V
+LIST_COLS = PAIR // 16
+
+
+def tile_picked_deform_lin_silu_def_e_kernel(tc, xT, w, b, offs, out):
+    nc = tc.nc
+
+    def on_vector(dst, src):
+        nc.vector.tensor_copy(out=dst, in_=src)
+
+    def on_scalar(dst, src):
+        nc.scalar.activation(out=dst, in_=src, func=ACT.Copy)
+
+    with ExitStack() as ctx:
+        keep = ctx.enter_context(tc.tile_pool(name="keep", bufs=1))
+        stage = ctx.enter_context(tc.tile_pool(name="stage", bufs=3))
+        ring = ctx.enter_context(tc.tile_pool(name="ring", bufs=6))
+        psum = ctx.enter_context(tc.psum_pool(name="psum", bufs=1))
+
+        offsets = keep.tile([P, T // 16], U16, name="offsets")
+        bias = keep.tile([P, M_TILES], F32, name="bias")
+
+        warm_in = keep.tile([P, 1], F32, name="warm_in")
+        warm_out = keep.tile([P, 1], F32, name="warm_out")
+        nc.vector.memset(warm_in[:], 0.0)
+        nc.scalar.activation(out=warm_out[:], in_=warm_in[:], func=ACT.Silu)
+
+        x_words = [keep.tile([P, T], U32, name=f"x_words{a}", align_bytes=64) for a in range(PASSES)]
+        x_scales = [keep.tile([P, T], U8, name=f"x_scales{a}", align_bytes=64) for a in range(PASSES)]
+        for a in range(PASSES):
+            nc.gpsimd.memset(x_scales[a][:], 0)
+
+        w_order = [(d, a) for a in range(PASSES) for d in range(D)]
+        stream = []
+        for a in range(PASSES):
+            stream.append(("x", a))
+            stream.append(("w", w_order[a]))
+        stream.extend(("w", da) for da in w_order[PASSES:])
+
+        def load(rows, name):
+            width = rows.shape[1]
+            raw = keep.tile([P, PACK, width], F32, name=name, align_bytes=64)
+            nc.sync.dma_start(
+                out=raw[:].rearrange("p j c -> p (j c)"),
+                in_=rows.rearrange("(p j) c -> p (j c)", j=PACK),
+            )
+            return raw
+
+        raws = {}
+        for n, (kind, key) in enumerate(stream):
+            if kind == "x":
+                raws[kind, key] = load(xT[key * K_PASS : (key + 1) * K_PASS, :], f"x_raw{key}")
+            else:
+                d, a = key
+                raws[kind, key] = load(w[d, a * K_PASS : (a + 1) * K_PASS, :], f"w_raw{d}{a}")
+            if n == 0:
+                nc.sync.dma_start(offsets[:], offs)
+        with nc.allow_non_contiguous_dma(reason="one bias value to a partition"):
+            nc.sync.dma_start(out=bias[:], in_=b.rearrange("(m p) o -> p (m o)", p=P))
+
+        def interleave(copy, raw, c0, c1, name, bufs):
+            grouped = stage.tile([P, c1 - c0, PACK], BF16, name=name, align_bytes=64, bufs=bufs)
+            copy(
+                grouped[:].rearrange("p (c i) j -> p c j i", i=RUN),
+                raw[:, :, c0:c1].rearrange("p j (c i) -> p c j i", i=RUN),
+            )
+            return grouped
+
+        def quantize(grouped, words, scales, c0, c1):
+            nc.vector.quantize_mx(
+                out=words[:, c0:c1].bitcast(FP8X4),
+                scales=scales[:, c0:c1],
+                in_=grouped[:].rearrange("p c j -> p (c j)"),
+            )
+
+        acc = [psum.tile([P, V], F32, name=f"acc{m}") for m in range(M_TILES)]
+        picked = {}
+
+        def multiply(d, a, words, scales, m):
+            g_words, g_scales = picked[a, d // 2]
+            v_cols = slice((d % 2) * V, (d % 2 + 1) * V)
+            m_cols = slice(m * P, (m + 1) * P)
+            nc.tensor.matmul_mx(
+                out=acc[m][:],
+                lhsT=words[:, m_cols].bitcast(FP8X4),
+                lhsT_scale=scales[:, m_cols],
+                rhs=g_words[:, v_cols].bitcast(FP8X4),
+                rhs_scale=g_scales[:, v_cols],
+                start=(d, a) == w_order[0],
+                stop=(d, a) == w_order[-1],
+            )
+
+        def finish(m):
+            y = keep.tile([P, V], F32, name=f"y{m}")
+            nc.scalar.activation(out=y[:], in_=acc[m][:], func=ACT.Silu, bias=bias[:, m : m + 1])
+            nc.sync.dma_start(out=out[m * P : (m + 1) * P, :], in_=y[:])
+
+        def do_x(a):
+            raw = raws["x", a]
+            half = T // 2
+            low = interleave(on_vector, raw, 0, half, "x_low", 2)
+            high = interleave(on_scalar, raw, half, T, "x_high", 2)
+            quantize(low, x_words[a], x_scales[a], 0, half)
+            quantize(high, x_words[a], x_scales[a], half, T)
+            for h in range(D // 2):
+                entries = offsets[:, h * LIST_COLS : (h + 1) * LIST_COLS]
+                g_words = keep.tile([P, PAIR], U32, name=f"g_words{a}{h}", align_bytes=64)
+                g_scales = keep.tile([P, PAIR], U8, name=f"g_scales{a}{h}", align_bytes=64)
+                nc.vector.tensor_copy(out=g_words[:], in_=x_words[a][:].indirect(entries))
+                nc.vector.tensor_copy(out=g_scales[:], in_=x_scales[a][:].indirect(entries))
+                picked[a, h] = (g_words, g_scales)
+
+        def do_w(d, a, low_copy):
+            raw = raws["w", (d, a)]
+            half = N // 2
+            words = ring.tile([P, N], U32, name="w_words", align_bytes=64)
+            scales = ring.tile([P, N], U8, name="w_scales", align_bytes=64)
+            high = interleave(on_scalar, raw, half, N, "w_high", 3)
+            low = interleave(low_copy, raw, 0, half, "w_low", 3)
+            quantize(low, words, scales, 0, half)
+            quantize(high, words, scales, half, N)
+            for m in range(M_TILES):
+                multiply(d, a, words, scales, m)
+
+        def do_last_w(d, a):
+            raw = raws["w", (d, a)]
+            words = ring.tile([P, N], U32, name="w_words", align_bytes=64)
+            scales = ring.tile([P, N], U8, name="w_scales", align_bytes=64)
+            part = {}
+
+            def cast(copy, m):
+                part[m] = interleave(copy, raw, m * P, (m + 1) * P, f"w_last{m}", 1)
+
+            def close(m):
+                quantize(part[m], words, scales, m * P, (m + 1) * P)
+                multiply(d, a, words, scales, m)
+                finish(m)
+
+            cast(on_vector, 0)
+            cast(on_scalar, 3)
+            cast(on_vector, 1)
+            close(0)
+            close(3)
+            cast(on_vector, 2)
+            close(1)
+            close(2)
+
+        for n, (kind, key) in enumerate(stream):
+            if kind == "x":
+                do_x(key)
+            elif key == w_order[-1]:
+                do_last_w(*key)
+            else:
+                do_w(*key, on_scalar if n < 2 * PASSES + 1 else on_vector)

@@ -1,6 +1,7 @@
 from contextlib import ExitStack
 
 import concourse.mybir as mybir
+from concourse.masks import make_identity
 
 K, T, D, V, N = 1536, 1024, 4, 256, 512
 FLOPS = 2 * D * K * N * V
@@ -21,6 +22,9 @@ M_TILES = N // P
 RUN = 4
 PAIR = 2 * V
 LIST_COLS = PAIR // 16
+HALF_T = T // 2
+X_VECTOR_COLS = 192
+W_VECTOR_COLS = 192
 
 
 def tile_picked_deform_lin_silu_def_e_kernel(tc, xT, w, b, offs, out):
@@ -48,43 +52,61 @@ def tile_picked_deform_lin_silu_def_e_kernel(tc, xT, w, b, offs, out):
 
         x_words = [keep.tile([P, T], U32, name=f"x_words{a}", align_bytes=64) for a in range(PASSES)]
         x_scales = [keep.tile([P, T], U8, name=f"x_scales{a}", align_bytes=64) for a in range(PASSES)]
+
+        b_rows = keep.tile([P, P], F32, name="b_rows")
+        identity = keep.tile([P, P], F32, name="identity")
+        b_turned = psum.tile([P, P], F32, name="b_turned")
+        nc.vector.memset(b_rows[:], 0.0)
+        nc.scalar.dma_start(out=b_rows[0:M_TILES, :], in_=b.rearrange("(m p) o -> m (p o)", p=P))
+        make_identity(nc, identity[:])
+        nc.tensor.transpose(b_turned[:], b_rows[:], identity[:])
+        nc.vector.tensor_copy(out=bias[:], in_=b_turned[:, 0:M_TILES])
+
         for a in range(PASSES):
             nc.gpsimd.memset(x_scales[a][:], 0)
 
-        w_order = [(d, a) for a in range(PASSES) for d in range(D)]
-        stream = []
-        for a in range(PASSES):
-            stream.append(("x", a))
-            stream.append(("w", w_order[a]))
-        stream.extend(("w", da) for da in w_order[PASSES:])
-
-        def load(rows, name):
-            width = rows.shape[1]
-            raw = keep.tile([P, PACK, width], F32, name=name, align_bytes=64)
-            nc.sync.dma_start(
-                out=raw[:].rearrange("p j c -> p (j c)"),
-                in_=rows.rearrange("(p j) c -> p (j c)", j=PACK),
-            )
+        def load(rows, c0, c1, name):
+            raw = keep.tile([P, PACK, c1 - c0], F32, name=name, align_bytes=64)
+            nc.sync.dma_start(out=raw[:], in_=rows[:, c0:c1].rearrange("(p j) c -> p j c", j=PACK))
             return raw
 
-        raws = {}
-        for n, (kind, key) in enumerate(stream):
-            if kind == "x":
-                raws[kind, key] = load(xT[key * K_PASS : (key + 1) * K_PASS, :], f"x_raw{key}")
-            else:
-                d, a = key
-                raws[kind, key] = load(w[d, a * K_PASS : (a + 1) * K_PASS, :], f"w_raw{d}{a}")
-            if n == 0:
-                nc.sync.dma_start(offsets[:], offs)
-        with nc.allow_non_contiguous_dma(reason="one bias value to a partition"):
-            nc.sync.dma_start(out=bias[:], in_=b.rearrange("(m p) o -> p (m o)", p=P))
+        def k_rows(a):
+            return slice(a * K_PASS, (a + 1) * K_PASS)
 
-        def interleave(copy, raw, c0, c1, name, bufs):
-            grouped = stage.tile([P, c1 - c0, PACK], BF16, name=name, align_bytes=64, bufs=bufs)
+        w_order = [(d, a) for a in range(PASSES) for d in range(D)]
+        x_raw, w_raw = {}, {}
+
+        def load_x(a):
+            raw = load(xT[k_rows(a), :], 0, T, f"x_raw{a}")
+            x_raw[a] = [raw[:, :, 0:HALF_T], raw[:, :, HALF_T:T]]
+
+        def load_w(d, a):
+            w_raw[d, a] = load(w[d, k_rows(a), :], 0, N, f"w_raw{d}{a}")
+
+        x_raw[0] = [load(xT[k_rows(0), :], c0, c0 + HALF_T, f"x_raw0{c0}") for c0 in (0, HALF_T)]
+        nc.sync.dma_start(offsets[:], offs)
+        load_w(*w_order[0])
+        load_x(1)
+        load_w(*w_order[1])
+        load_x(2)
+        for d, a in w_order[2:-1]:
+            load_w(d, a)
+        last_rows = w[D - 1, k_rows(PASSES - 1), :]
+        last_raw = [load(last_rows, c0, c1, f"w_raw_last{c0}") for c0, c1 in ((0, 2 * P), (2 * P, 3 * P), (3 * P, 4 * P))]
+
+        def interleave(copy, grouped, raw, c0, c1):
             copy(
-                grouped[:].rearrange("p (c i) j -> p c j i", i=RUN),
+                grouped[:, c0:c1, :].rearrange("p (c i) j -> p c j i", i=RUN),
                 raw[:, :, c0:c1].rearrange("p j (c i) -> p c j i", i=RUN),
             )
+
+        def interleave_shared(raw, vector_cols, name, bufs):
+            width = raw.shape[2]
+            grouped = stage.tile([P, width, PACK], BF16, name=name, align_bytes=64, bufs=bufs)
+            if vector_cols < width:
+                interleave(on_scalar, grouped, raw, vector_cols, width)
+            if vector_cols > 0:
+                interleave(on_vector, grouped, raw, 0, vector_cols)
             return grouped
 
         def quantize(grouped, words, scales, c0, c1):
@@ -117,12 +139,9 @@ def tile_picked_deform_lin_silu_def_e_kernel(tc, xT, w, b, offs, out):
             nc.sync.dma_start(out=out[m * P : (m + 1) * P, :], in_=y[:])
 
         def do_x(a):
-            raw = raws["x", a]
-            half = T // 2
-            low = interleave(on_vector, raw, 0, half, "x_low", 2)
-            high = interleave(on_scalar, raw, half, T, "x_high", 2)
-            quantize(low, x_words[a], x_scales[a], 0, half)
-            quantize(high, x_words[a], x_scales[a], half, T)
+            halves = [interleave_shared(raw, X_VECTOR_COLS, "x_grouped", 4) for raw in x_raw[a]]
+            for h, grouped in enumerate(halves):
+                quantize(grouped, x_words[a], x_scales[a], h * HALF_T, (h + 1) * HALF_T)
             for h in range(D // 2):
                 entries = offsets[:, h * LIST_COLS : (h + 1) * LIST_COLS]
                 g_words = keep.tile([P, PAIR], U32, name=f"g_words{a}{h}", align_bytes=64)
@@ -131,45 +150,57 @@ def tile_picked_deform_lin_silu_def_e_kernel(tc, xT, w, b, offs, out):
                 nc.vector.tensor_copy(out=g_scales[:], in_=x_scales[a][:].indirect(entries))
                 picked[a, h] = (g_words, g_scales)
 
-        def do_w(d, a, low_copy):
-            raw = raws["w", (d, a)]
-            half = N // 2
+        def w_codes():
             words = ring.tile([P, N], U32, name="w_words", align_bytes=64)
             scales = ring.tile([P, N], U8, name="w_scales", align_bytes=64)
-            high = interleave(on_scalar, raw, half, N, "w_high", 3)
-            low = interleave(low_copy, raw, 0, half, "w_low", 3)
-            quantize(low, words, scales, 0, half)
-            quantize(high, words, scales, half, N)
+            return words, scales
+
+        def do_w(d, a, vector_cols):
+            words, scales = w_codes()
+            grouped = interleave_shared(w_raw[d, a], vector_cols, "w_grouped", 4)
+            quantize(grouped, words, scales, 0, N)
+            for m in range(M_TILES):
+                multiply(d, a, words, scales, m)
+
+        def do_w_halves(d, a):
+            words, scales = w_codes()
+            raw = w_raw[d, a]
+            high = interleave_shared(raw[:, :, N // 2 : N], 0, "w_high", 1)
+            low = interleave_shared(raw[:, :, 0 : N // 2], N // 2, "w_low", 1)
+            quantize(low, words, scales, 0, N // 2)
+            quantize(high, words, scales, N // 2, N)
             for m in range(M_TILES):
                 multiply(d, a, words, scales, m)
 
         def do_last_w(d, a):
-            raw = raws["w", (d, a)]
-            words = ring.tile([P, N], U32, name="w_words", align_bytes=64)
-            scales = ring.tile([P, N], U8, name="w_scales", align_bytes=64)
+            words, scales = w_codes()
             part = {}
 
-            def cast(copy, m):
-                part[m] = interleave(copy, raw, m * P, (m + 1) * P, f"w_last{m}", 1)
+            def cast(m, raw, vector_cols):
+                part[m] = interleave_shared(raw, vector_cols, f"w_last{m}", 1)
 
             def close(m):
                 quantize(part[m], words, scales, m * P, (m + 1) * P)
                 multiply(d, a, words, scales, m)
                 finish(m)
 
-            cast(on_vector, 0)
-            cast(on_scalar, 3)
-            cast(on_vector, 1)
+            cast(0, last_raw[0][:, :, 0:P], P)
+            cast(1, last_raw[0][:, :, P : 2 * P], 0)
+            cast(2, last_raw[1], 0)
             close(0)
-            close(3)
-            cast(on_vector, 2)
             close(1)
+            cast(3, last_raw[2], P)
             close(2)
+            close(3)
 
-        for n, (kind, key) in enumerate(stream):
-            if kind == "x":
-                do_x(key)
-            elif key == w_order[-1]:
-                do_last_w(*key)
-            else:
-                do_w(*key, on_scalar if n < 2 * PASSES + 1 else on_vector)
+        do_x(0)
+        do_w(*w_order[0], 0)
+        do_x(1)
+        do_w(*w_order[1], 0)
+        do_x(2)
+        for d, a in w_order[2:5]:
+            do_w(d, a, 0)
+        for d, a in w_order[5:-2]:
+            do_w(d, a, W_VECTOR_COLS)
+        do_w_halves(*w_order[-2])
+        do_last_w(*w_order[-1])

@@ -8,6 +8,7 @@ FLOPS = 2 * D * K * N * V
 
 F32 = mybir.dt.float32
 BF16 = mybir.dt.bfloat16
+I32 = mybir.dt.int32
 U32 = mybir.dt.uint32
 U16 = mybir.dt.uint16
 U8 = mybir.dt.uint8
@@ -23,8 +24,6 @@ RUN = 4
 PAIR = 2 * V
 LIST_COLS = PAIR // 16
 HALF_T = T // 2
-X_VECTOR_COLS = 192
-W_VECTOR_COLS = 192
 
 
 def tile_picked_deform_lin_silu_def_e_kernel(tc, xT, w, b, offs, out):
@@ -63,7 +62,7 @@ def tile_picked_deform_lin_silu_def_e_kernel(tc, xT, w, b, offs, out):
         nc.vector.tensor_copy(out=bias[:], in_=b_turned[:, 0:M_TILES])
 
         for a in range(PASSES):
-            nc.gpsimd.memset(x_scales[a][:], 0)
+            nc.gpsimd.memset(x_scales[a][:].bitcast(I32), 0)
 
         def load(rows, c0, c1, name):
             raw = keep.tile([P, PACK, c1 - c0], F32, name=name, align_bytes=64)
@@ -138,8 +137,8 @@ def tile_picked_deform_lin_silu_def_e_kernel(tc, xT, w, b, offs, out):
             nc.scalar.activation(out=y[:], in_=acc[m][:], func=ACT.Silu, bias=bias[:, m : m + 1])
             nc.sync.dma_start(out=out[m * P : (m + 1) * P, :], in_=y[:])
 
-        def do_x(a):
-            halves = [interleave_shared(raw, X_VECTOR_COLS, "x_grouped", 4) for raw in x_raw[a]]
+        def do_x(a, vector_cols):
+            halves = [interleave_shared(raw, vector_cols, "x_grouped", 4) for raw in x_raw[a]]
             for h, grouped in enumerate(halves):
                 quantize(grouped, x_words[a], x_scales[a], h * HALF_T, (h + 1) * HALF_T)
             for h in range(D // 2):
@@ -193,14 +192,15 @@ def tile_picked_deform_lin_silu_def_e_kernel(tc, xT, w, b, offs, out):
             close(2)
             close(3)
 
-        do_x(0)
+        do_x(0, 256)
         do_w(*w_order[0], 0)
-        do_x(1)
+        do_x(1, 192)
         do_w(*w_order[1], 0)
-        do_x(2)
-        for d, a in w_order[2:5]:
-            do_w(d, a, 0)
+        do_x(2, 192)
+        do_w(*w_order[2], 0)
+        do_w(*w_order[3], 0)
+        do_w(*w_order[4], 128)
         for d, a in w_order[5:-2]:
-            do_w(d, a, W_VECTOR_COLS)
+            do_w(d, a, 256)
         do_w_halves(*w_order[-2])
         do_last_w(*w_order[-1])

from contextlib import ExitStack

import concourse.mybir as mybir
from concourse.masks import make_identity

K, T, D, V, N = 1536, 1024, 4, 256, 512
FLOPS = 2 * D * K * N * V

F32 = mybir.dt.float32
BF16 = mybir.dt.bfloat16
I32 = mybir.dt.int32
U32 = mybir.dt.uint32
U16 = mybir.dt.uint16
U8 = mybir.dt.uint8
FP8X4 = mybir.dt.float8_e4m3fn_x4
ACT = mybir.ActivationFunctionType

P = 128
PACK = 4
K_PASS = P * PACK
PASSES = K // K_PASS
M_TILES = N // P
RUN = 4
PAIR = 2 * V
LIST_COLS = PAIR // 16
HALF_T = T // 2


def tile_picked_deform_lin_silu_def_e_kernel(tc, xT, w, b, offs, out):
    nc = tc.nc

    def on_vector(dst, src):
        nc.vector.tensor_copy(out=dst, in_=src)

    def on_scalar(dst, src):
        nc.scalar.activation(out=dst, in_=src, func=ACT.Copy)

    with ExitStack() as ctx:
        keep = ctx.enter_context(tc.tile_pool(name="keep", bufs=1))
        stage = ctx.enter_context(tc.tile_pool(name="stage", bufs=3))
        ring = ctx.enter_context(tc.tile_pool(name="ring", bufs=6))
        psum = ctx.enter_context(tc.psum_pool(name="psum", bufs=1))

        offsets = keep.tile([P, T // 16], U16, name="offsets")
        bias = keep.tile([P, M_TILES], F32, name="bias")

        warm_in = keep.tile([P, 1], F32, name="warm_in")
        warm_out = keep.tile([P, 1], F32, name="warm_out")
        nc.vector.memset(warm_in[:], 0.0)
        nc.scalar.activation(out=warm_out[:], in_=warm_in[:], func=ACT.Silu)

        x_words = [keep.tile([P, T], U32, name=f"x_words{a}", align_bytes=64) for a in range(PASSES)]
        x_scales = [keep.tile([P, T], U8, name=f"x_scales{a}", align_bytes=64) for a in range(PASSES)]

        b_rows = keep.tile([P, P], F32, name="b_rows")
        identity = keep.tile([P, P], F32, name="identity")
        b_turned = psum.tile([P, P], F32, name="b_turned")
        nc.vector.memset(b_rows[:], 0.0)
        nc.scalar.dma_start(out=b_rows[0:M_TILES, :], in_=b.rearrange("(m p) o -> m (p o)", p=P))
        make_identity(nc, identity[:])
        nc.tensor.transpose(b_turned[:], b_rows[:], identity[:])
        nc.vector.tensor_copy(out=bias[:], in_=b_turned[:, 0:M_TILES])

        for a in range(PASSES):
            nc.gpsimd.memset(x_scales[a][:].bitcast(I32), 0)

        def load(rows, c0, c1, name):
            raw = keep.tile([P, PACK, c1 - c0], F32, name=name, align_bytes=64)
            nc.sync.dma_start(out=raw[:], in_=rows[:, c0:c1].rearrange("(p j) c -> p j c", j=PACK))
            return raw

        def k_rows(a):
            return slice(a * K_PASS, (a + 1) * K_PASS)

        w_order = [(d, a) for a in range(PASSES) for d in range(D)]
        x_raw, w_raw = {}, {}

        def load_x(a):
            raw = load(xT[k_rows(a), :], 0, T, f"x_raw{a}")
            x_raw[a] = [raw[:, :, 0:HALF_T], raw[:, :, HALF_T:T]]

        def load_w(d, a):
            w_raw[d, a] = load(w[d, k_rows(a), :], 0, N, f"w_raw{d}{a}")

        x_raw[0] = [load(xT[k_rows(0), :], c0, c0 + HALF_T, f"x_raw0{c0}") for c0 in (0, HALF_T)]
        nc.sync.dma_start(offsets[:], offs)
        load_w(*w_order[0])
        load_x(1)
        load_w(*w_order[1])
        load_x(2)
        for d, a in w_order[2:-1]:
            load_w(d, a)
        last_rows = w[D - 1, k_rows(PASSES - 1), :]
        last_raw = [load(last_rows, c0, c1, f"w_raw_last{c0}") for c0, c1 in ((0, 2 * P), (2 * P, 3 * P), (3 * P, 4 * P))]

        def interleave(copy, grouped, raw, c0, c1):
            copy(
                grouped[:, c0:c1, :].rearrange("p (c i) j -> p c j i", i=RUN),
                raw[:, :, c0:c1].rearrange("p j (c i) -> p c j i", i=RUN),
            )

        def interleave_shared(raw, vector_cols, name, bufs):
            width = raw.shape[2]
            grouped = stage.tile([P, width, PACK], BF16, name=name, align_bytes=64, bufs=bufs)
            if vector_cols < width:
                interleave(on_scalar, grouped, raw, vector_cols, width)
            if vector_cols > 0:
                interleave(on_vector, grouped, raw, 0, vector_cols)
            return grouped

        def quantize(grouped, words, scales, c0, c1):
            nc.vector.quantize_mx(
                out=words[:, c0:c1].bitcast(FP8X4),
                scales=scales[:, c0:c1],
                in_=grouped[:].rearrange("p c j -> p (c j)"),
            )

        acc = [psum.tile([P, V], F32, name=f"acc{m}") for m in range(M_TILES)]
        picked = {}

        def multiply(d, a, words, scales, m):
            g_words, g_scales = picked[a, d // 2]
            v_cols = slice((d % 2) * V, (d % 2 + 1) * V)
            m_cols = slice(m * P, (m + 1) * P)
            nc.tensor.matmul_mx(
                out=acc[m][:],
                lhsT=words[:, m_cols].bitcast(FP8X4),
                lhsT_scale=scales[:, m_cols],
                rhs=g_words[:, v_cols].bitcast(FP8X4),
                rhs_scale=g_scales[:, v_cols],
                start=(d, a) == w_order[0],
                stop=(d, a) == w_order[-1],
            )

        def finish(m):
            y = keep.tile([P, V], F32, name=f"y{m}")
            nc.scalar.activation(out=y[:], in_=acc[m][:], func=ACT.Silu, bias=bias[:, m : m + 1])
            nc.sync.dma_start(out=out[m * P : (m + 1) * P, :], in_=y[:])

        def do_x(a, vector_cols):
            halves = [interleave_shared(raw, vector_cols, "x_grouped", 4) for raw in x_raw[a]]
            for h, grouped in enumerate(halves):
                quantize(grouped, x_words[a], x_scales[a], h * HALF_T, (h + 1) * HALF_T)
            for h in range(D // 2):
                entries = offsets[:, h * LIST_COLS : (h + 1) * LIST_COLS]
                g_words = keep.tile([P, PAIR], U32, name=f"g_words{a}{h}", align_bytes=64)
                g_scales = keep.tile([P, PAIR], U8, name=f"g_scales{a}{h}", align_bytes=64)
                nc.vector.tensor_copy(out=g_words[:], in_=x_words[a][:].indirect(entries))
                nc.vector.tensor_copy(out=g_scales[:], in_=x_scales[a][:].indirect(entries))
                picked[a, h] = (g_words, g_scales)

        def w_codes():
            words = ring.tile([P, N], U32, name="w_words", align_bytes=64)
            scales = ring.tile([P, N], U8, name="w_scales", align_bytes=64)
            return words, scales

        def do_w(d, a, vector_cols):
            words, scales = w_codes()
            grouped = interleave_shared(w_raw[d, a], vector_cols, "w_grouped", 4)
            quantize(grouped, words, scales, 0, N)
            for m in range(M_TILES):
                multiply(d, a, words, scales, m)

        def do_w_halves(d, a):
            words, scales = w_codes()
            raw = w_raw[d, a]
            high = interleave_shared(raw[:, :, N // 2 : N], 0, "w_high", 1)
            low = interleave_shared(raw[:, :, 0 : N // 2], N // 2, "w_low", 1)
            quantize(low, words, scales, 0, N // 2)
            quantize(high, words, scales, N // 2, N)
            for m in range(M_TILES):
                multiply(d, a, words, scales, m)

        def do_last_w(d, a):
            words, scales = w_codes()
            part = {}

            def cast(m, raw, vector_cols):
                part[m] = interleave_shared(raw, vector_cols, f"w_last{m}", 1)

            def close(m):
                quantize(part[m], words, scales, m * P, (m + 1) * P)
                multiply(d, a, words, scales, m)
                finish(m)

            cast(0, last_raw[0][:, :, 0:P], P)
            cast(1, last_raw[0][:, :, P : 2 * P], 0)
            cast(2, last_raw[1], 0)
            close(0)
            close(1)
            cast(3, last_raw[2], P)
            close(2)
            close(3)

        do_x(0, 256)
        do_w(*w_order[0], 0)
        do_x(1, 192)
        do_w(*w_order[1], 0)
        do_x(2, 192)
        do_w(*w_order[2], 0)
        do_w(*w_order[3], 0)
        do_w(*w_order[4], 128)
        for d, a in w_order[5:-2]:
            do_w(d, a, 256)
        do_w_halves(*w_order[-2])
        do_last_w(*w_order[-1])
